import numpy as np
import ml_dtypes


def mxq(x, axis, fmt="e4m3"):
    dtype, down = {"e4m3": (ml_dtypes.float8_e4m3fn, 7), "e5m2": (ml_dtypes.float8_e5m2, 14)}[fmt]
    v = np.moveaxis(np.asarray(x, np.float32).astype(ml_dtypes.bfloat16).astype(np.float64), axis, -1)
    blocks = v.reshape(v.shape[:-1] + (-1, 32))
    amax = np.abs(blocks).max(-1, keepdims=True)
    byte = np.maximum(np.where(amax > 0, np.frexp(amax)[1] - 1 + 127, 0) - down, 1)
    scale = np.exp2(byte - 127.0)
    codes = (blocks / scale).astype(np.float32).astype(dtype).astype(np.float64)
    return np.moveaxis((codes * scale).reshape(v.shape), -1, axis)


WIDE = False


def mx_kscale(k):
    if not WIDE:
        return np.ones(k)
    levels = np.array([30, -30])
    if k % 512:
        return np.exp2(np.random.permutation(np.resize(levels, k // 32))).repeat(32)
    a = np.empty((k // 512, 16))
    for p in range(k // 512):
        a[p, :8] = np.random.permutation(np.resize(levels, 8))
        for g in range(8):
            far = levels[np.abs(levels - a[p, g]) >= 10]
            a[p, g + 8] = far[np.random.randint(len(far))]
    return np.exp2(a.ravel()).repeat(32)


def f64(x):
    return np.asarray(x).astype(np.float64)


def striped(idx):
    return np.tile(np.asarray(idx).reshape(-1, 16).T, (8, 1)).astype(np.uint16)


def unstriped(offs):
    return offs[:16].T.reshape(-1).astype(np.int64)


E2M1 = np.array([0.0, 0.5, 1.0, 1.5, 2.0, 3.0, 4.0, 6.0, -0.0, -0.5, -1.0, -1.5, -2.0, -3.0, -4.0, -6.0])


def pack_weight(w, fmt):
    k, n = w.shape
    w = f64(np.asarray(w, np.float32).astype(ml_dtypes.bfloat16)).reshape(k // 32, 32, n)
    amax = np.abs(w).max(1)
    if fmt in ("e4m3", "e5m2"):
        byte = np.frexp(amax)[1] - 1 + 127 - (7 if fmt == "e4m3" else 14)
    else:
        mant, ex = np.frexp(amax / 6.0)
        byte = np.where(mant > 0.5, ex, ex - 1) + 127
    byte = np.clip(np.where(amax > 0, byte, 1), 1, 254)
    scaled = (w * np.exp2(127.0 - byte)[:, None, :]).reshape(k, n).astype(np.float32)
    by_word = np.ascontiguousarray(scaled.reshape(k // 512, 128, 4, n).transpose(0, 1, 3, 2))
    if fmt in ("e4m3", "e5m2"):
        words = by_word.astype(ml_dtypes.float8_e4m3fn if fmt == "e4m3" else ml_dtypes.float8_e5m2).view(np.uint8)
    else:
        c = by_word.astype(ml_dtypes.float4_e2m1fn).view(np.uint8) & 0xF
        words = (c[..., 0::2] | (c[..., 1::2] << 4)).reshape(k // 512, 128, 2 * n)
    return np.ascontiguousarray(words), np.ascontiguousarray(byte.astype(np.uint8).reshape(k // 512, 16, n))


def unpack_weight(words, scales, fmt):
    g, _, n = scales.shape
    words = np.ascontiguousarray(words).reshape(g, 128, n, -1)
    if fmt in ("e4m3", "e5m2"):
        vals = words.view(ml_dtypes.float8_e4m3fn if fmt == "e4m3" else ml_dtypes.float8_e5m2).astype(np.float64)
    else:
        nib = np.empty((g, 128, n, 4), np.uint8)
        nib[..., 0::2] = words & 0xF
        nib[..., 1::2] = words >> 4
        vals = E2M1[nib]
    vals = vals * np.repeat(np.exp2(scales.astype(np.float64) - 127.0), 8, axis=1)[..., None]
    return vals.transpose(0, 1, 3, 2).reshape(g * 512, n)


def bf(x):
    return np.asarray(x, np.float32).astype(ml_dtypes.bfloat16)


def planes(Y):
    r, m = Y.shape
    b = f64(bf(Y)).reshape(r // 32, 32, m)
    amax = np.abs(b).max(1)
    byte = np.clip(np.where(amax > 0, np.frexp(amax)[1] - 1 + 127 - 7, 1), 1, 254)
    codes = (b * np.exp2(127.0 - byte)[:, None, :]).reshape(r, m).astype(np.float32).astype(ml_dtypes.float8_e4m3fn).view(np.uint8)
    words = codes.reshape(r // 512, 128, 4, m).transpose(0, 1, 3, 2)
    return np.ascontiguousarray(words), np.ascontiguousarray(byte.astype(np.uint8).reshape(r // 512, 16, m))


K, T, Z, J, R, C, O, N, E = 512, 1024, 1024, 256, 512, 512, 256, 512, 1024


def setup_inputs():
    n = np.random.standard_normal
    idx = np.random.permutation(T)[:J]
    idx2 = np.random.permutation(Z)[:J]
    idx3 = np.random.permutation(C)[:J]
    idx4 = np.random.permutation(C)[:J]
    idx5 = np.random.permutation(C)[:O]
    idx6 = np.random.permutation(C)[:O]
    idx7 = np.random.permutation(E)[:O]
    fk = mx_kscale(K)
    fr = mx_kscale(R)
    xtp = pack_weight(n((K, T)) / fk[:, None], "e5m2")
    xop = pack_weight(n((K, Z)) / fk[:, None], "e4m3")
    wp = pack_weight(n((K, R)) * 1 / np.sqrt(K) * fk[:, None] * fr, "e2m1")
    w2p = pack_weight(n((K, R)) * 1 / np.sqrt(K) * fk[:, None] * fr, "e5m2")
    wbp = pack_weight(n((R, N)) * 1 / np.sqrt(R) / fr[:, None], "e2m1")
    return {
        "xt_words": xtp[0],
        "xt_scales": xtp[1],
        "xo_words": xop[0],
        "xo_scales": xop[1],
        "w_words": wp[0],
        "w_scales": wp[1],
        "w2_words": w2p[0],
        "w2_scales": w2p[1],
        "wb_words": wbp[0],
        "wb_scales": wbp[1],
        "tz": (n((N, E))).astype(np.float32),
        "offs": striped(idx),
        "offs2": striped(idx2),
        "offs3": striped(idx3),
        "offs4": striped(idx4),
        "offs5": striped(idx5),
        "offs6": striped(idx6),
        "offs7": striped(idx7),
    }


def reference(xt_words, xt_scales, xo_words, xo_scales, w_words, w_scales, w2_words, w2_scales, wb_words, wb_scales, tz, offs, offs2, offs3, offs4, offs5, offs6, offs7):
    idx = unstriped(offs)
    idx2 = unstriped(offs2)
    idx3 = unstriped(offs3)
    idx4 = unstriped(offs4)
    idx5 = unstriped(offs5)
    idx6 = unstriped(offs6)
    idx7 = unstriped(offs7)
    xtu = unpack_weight(xt_words, xt_scales, "e5m2")
    xou = unpack_weight(xo_words, xo_scales, "e4m3")
    wu = unpack_weight(w_words, w_scales, "e2m1")
    w2u = unpack_weight(w2_words, w2_scales, "e5m2")
    wbu = unpack_weight(wb_words, wb_scales, "e2m1")
    xtidxg = xtu[:, idx]
    xoidx2g = xou[:, idx2]
    a = wu.T @ xtidxg + w2u.T @ xoidx2g
    b = w2u.T @ xtidxg + wu.T @ xoidx2g
    pw = np.zeros((R, C))
    pw[:, idx3] = a
    pv = np.zeros((R, C))
    pv[:, idx4] = b
    hid = np.abs(pw[:, idx5] - pv[:, idx6])
    hidq = mxq(hid, 0, "e4m3")
    p = wbu.T @ hidq
    y = p + f64(tz)[:, idx7]
    words, scales = planes(y)
    return y, words, scales

@@ -1,0 +1,193 @@
+from contextlib import ExitStack
+
+import concourse.mybir as mybir
+
+K, T, Z, J, R, C, O, N, E = 512, 1024, 1024, 256, 512, 512, 256, 512, 1024
+FLOPS = 2 * K * R * J * 4 + 2 * R * N * O
+
+F32 = mybir.dt.float32
+BF16 = mybir.dt.bfloat16
+I32 = mybir.dt.int32
+U32 = mybir.dt.uint32
+U16 = mybir.dt.uint16
+U8 = mybir.dt.uint8
+E4M3 = mybir.dt.float8_e4m3fn_x4
+E5M2 = mybir.dt.float8_e5m2_x4
+E2M1 = mybir.dt.float4_e2m1fn_x4
+ACT = mybir.ActivationFunctionType
+ALU = mybir.AluOpType
+
+P = 128
+PACK = 4
+QUADS = 4
+HALVES = 2
+HALF = O // HALVES
+PER_COLUMN = 16
+
+
+def tile_list_crossed_twoboards_one_tabled_pl_kernel(
+    tc, xt_words, xt_scales, xo_words, xo_scales, w_words, w_scales, w2_words, w2_scales,
+    wb_words, wb_scales, tz, offs, offs2, offs3, offs4, offs5, offs6, offs7, out_0, out_1, out_2,
+):
+    nc = tc.nc
+    with ExitStack() as ctx:
+        held = ctx.enter_context(tc.tile_pool(name="held", bufs=1))
+        psum = ctx.enter_context(tc.psum_pool(name="psum", bufs=1))
+
+        def sbuf(name, shape, dtype, tag=None):
+            return held.tile(shape, dtype, name=name, tag=tag or name, align_bytes=64)
+
+        def load_list(name, source):
+            entries = held.tile([P, J // PER_COLUMN], U16, name=name)
+            nc.sync.dma_start(entries[:], source)
+            return entries
+
+        def load_words(name, source, tag=None):
+            words = source.bitcast(I32)
+            raw = sbuf(name, [P, words.shape[1]], I32, tag)
+            nc.sync.dma_start(raw[:], words)
+            return raw
+
+        def load_scales(plane, source):
+            for q in range(QUADS):
+                queue = nc.scalar if q % 2 == 0 else nc.sync
+                queue.dma_start(plane[32 * q : 32 * q + 4, :].bitcast(I32), source[0, 4 * q : 4 * q + 4, :].bitcast(I32))
+
+        def deal(copy, dealt, raw):
+            copy(dealt.rearrange("p (t m) -> p m t", t=PACK), raw.rearrange("p (m t) -> p m t", t=PACK))
+
+        xt_plane = sbuf("xt_plane", [P, T], U8)
+        xo_plane = sbuf("xo_plane", [P, Z], U8)
+        ww_plane = sbuf("ww_plane", [P, 2 * R], U8)
+        wb_plane = sbuf("wb_plane", [P, N], U8)
+        for plane in (xt_plane, ww_plane, xo_plane, wb_plane):
+            nc.vector.memset(plane[:].bitcast(I32), 0)
+
+        xt_raw = load_words("xt_raw", xt_words[0].rearrange("p c b -> p (c b)"), "wide0")
+        idx = load_list("idx", offs)
+        w2_raw = load_words("w2_raw", w2_words[0].rearrange("p c b -> p (c b)"), "wide2")
+        w_raw = load_words("w_raw", w_words[0], "wide3")
+        load_scales(xt_plane[:], xt_scales)
+        load_scales(ww_plane[:, 0:R], w_scales)
+        load_scales(ww_plane[:, R : 2 * R], w2_scales)
+        xo_raw = load_words("xo_raw", xo_words[0].rearrange("p c b -> p (c b)"), "wide1")
+        idx2 = load_list("idx2", offs2)
+        load_scales(xo_plane[:], xo_scales)
+        idx3 = load_list("idx3", offs3)
+        idx4 = load_list("idx4", offs4)
+        idx5 = load_list("idx5", offs5)
+        idx6 = load_list("idx6", offs6)
+        wb_raw = load_words("wb_raw", wb_words[0])
+        load_scales(wb_plane[:], wb_scales)
+        idx7 = load_list("idx7", offs7)
+
+        pw = [sbuf("pw%d" % t, [P, C], F32) for t in range(PACK)]
+        pv = [sbuf("pv%d" % t, [P, C], F32) for t in range(PACK)]
+        for t in range(PACK):
+            nc.vector.memset(pv[t][:], 0.0)
+            nc.vector.memset(pw[t][:], 0.0)
+
+        w_codes = sbuf("w_codes", [P, 2 * R], U8)
+        w2_codes = sbuf("w2_codes", [P, R], U32)
+        ww_exps = sbuf("ww_exps", [P, 2 * R], U8)
+        deal(nc.scalar.copy, w2_codes[:], w2_raw[:].bitcast(U32))
+        deal(nc.scalar.copy, w_codes[:].bitcast(U16), w_raw[:].bitcast(U16))
+
+        xt_codes = sbuf("xt_codes", [P, J], U32)
+        xt_exps = sbuf("xt_exps", [P, J], U8)
+        xo_codes = sbuf("xo_codes", [P, J], U32)
+        xo_exps = sbuf("xo_exps", [P, J], U8)
+        nc.vector.tensor_copy(xt_codes[:], xt_raw[:].bitcast(U32).indirect(idx[:]))
+        nc.vector.tensor_copy(xt_exps[:], xt_plane[:].indirect(idx[:]))
+        nc.vector.tensor_copy(
+            ww_exps[:].rearrange("p (u t m) -> p u m t", u=2, t=PACK),
+            ww_plane[:].rearrange("p (u m t) -> p u m t", u=2, t=PACK),
+        )
+        nc.vector.tensor_copy(xo_codes[:], xo_raw[:].bitcast(U32).indirect(idx2[:]))
+        nc.vector.tensor_copy(xo_exps[:], xo_plane[:].indirect(idx2[:]))
+
+        tz_rows = tz.rearrange("(p t) e -> p t e", t=PACK)
+        tz_raw = []
+        for t in range(PACK):
+            rows = sbuf("tz_raw%d" % t, [P, E], F32, "wide%d" % t)
+            nc.sync.dma_start(rows[:], tz_rows[:, t, :])
+            tz_raw.append(rows)
+
+        xt_operand = (xt_codes[:].bitcast(E5M2), xt_exps[:])
+        xo_operand = (xo_codes[:].bitcast(E4M3), xo_exps[:])
+
+        def product(bank, stationary, moving, start, stop):
+            nc.tensor.matmul_mx(
+                out=bank, lhsT=stationary[0], lhsT_scale=stationary[1],
+                rhs=moving[0], rhs_scale=moving[1], start=start, stop=stop,
+            )
+
+        pw_read = sbuf("pw_read", [P, PACK, O], F32)
+        diff = sbuf("diff", [P, PACK, O], F32)
+        tz_read = sbuf("tz_read", [P, PACK, O], F32)
+        wb_codes = sbuf("wb_codes", [P, 2 * N], U8)
+        wb_exps = sbuf("wb_exps", [P, N], U8)
+
+        def read_boards(t, first, count):
+            columns = slice(first // PER_COLUMN, (first + count) // PER_COLUMN)
+            reads = slice(first, first + count)
+            nc.scalar.activation(pw_read[:, t, reads], pw[t][:].indirect(idx5[:, columns]), ACT.Copy)
+            nc.vector.tensor_tensor(diff[:, t, reads], pv[t][:].indirect(idx6[:, columns]), pw_read[:, t, reads], ALU.subtract)
+
+        for t in range(PACK):
+            w_slice = (w_codes[:, 2 * P * t : 2 * P * (t + 1)].bitcast(E2M1), ww_exps[:, P * t : P * (t + 1)])
+            w2_slice = (w2_codes[:, P * t : P * (t + 1)].bitcast(E5M2), ww_exps[:, R + P * t : R + P * (t + 1)])
+            a_bank = psum.tile([P, J], F32, name="a_bank%d" % t, tag="bank%d" % (2 * t))
+            b_bank = psum.tile([P, J], F32, name="b_bank%d" % t, tag="bank%d" % (2 * t + 1))
+            product(b_bank[:], w2_slice, xt_operand, True, False)
+            product(a_bank[:], w_slice, xt_operand, True, False)
+            product(b_bank[:], w_slice, xo_operand, False, True)
+            product(a_bank[:], w2_slice, xo_operand, False, True)
+            a_sums = sbuf("a_sums%d" % t, [P, J], F32)
+            b_sums = sbuf("b_sums%d" % t, [P, J], F32)
+            nc.scalar.activation(b_sums[:], b_bank[:], ACT.Copy)
+            nc.scalar.activation(a_sums[:], a_bank[:], ACT.Copy)
+            nc.vector.tensor_copy(pv[t][:].indirect(idx4[:]), b_sums[:])
+            nc.scalar.activation(pw[t][:].indirect(idx3[:]), a_sums[:], ACT.Copy)
+            if t < PACK - 1:
+                read_boards(t, 0, O)
+
+        deal(nc.scalar.copy, wb_codes[:].bitcast(U16), wb_raw[:].bitcast(U16))
+        deal(nc.vector.tensor_copy, wb_exps[:], wb_plane[:])
+        for t in range(PACK):
+            nc.vector.tensor_copy(tz_read[:, t, :], tz_raw[t][:].indirect(idx7[:]))
+
+        def woven(tile_ap):
+            return tile_ap.rearrange("p (c i t) -> p c t i", i=4, t=PACK)
+
+        def rows_of(slices_ap):
+            return slices_ap.rearrange("p t (c i) -> p c t i", i=4)
+
+        hid_codes = sbuf("hid_codes", [P, O], U32)
+        hid_exps = sbuf("hid_exps", [P, O], U8)
+        y_codes = sbuf("y_codes", [P, O], I32)
+        y_exps = sbuf("y_exps", [P, O], U8)
+        out_rows = out_0.rearrange("(p t) o -> p t o", t=PACK)
+        out_codes = out_1[0].rearrange("p c b -> p (c b)").bitcast(I32)
+        for h in range(HALVES):
+            read_boards(PACK - 1, h * HALF, HALF)
+        for h in range(HALVES):
+            reads = slice(h * HALF, (h + 1) * HALF)
+            hid = sbuf("hid%d" % h, [P, PACK * HALF], BF16)
+            nc.scalar.activation(woven(hid[:]), rows_of(diff[:, :, reads]), ACT.Abs)
+            nc.vector.quantize_mx(out=hid_codes[:, reads].bitcast(E4M3), scales=hid_exps[:, reads], in_=hid[:])
+            p_bank = psum.tile([P, PACK, HALF], F32, name="p_bank%d" % h, tag="bank%d" % h)
+            hid_operand = (hid_codes[:, reads].bitcast(E4M3), hid_exps[:, reads])
+            for t in range(PACK):
+                wb_slice = (wb_codes[:, 2 * P * t : 2 * P * (t + 1)].bitcast(E2M1), wb_exps[:, P * t : P * (t + 1)])
+                product(p_bank[:, t, :], wb_slice, hid_operand, True, True)
+            y = sbuf("y%d" % h, [P, PACK, HALF], F32)
+            nc.vector.tensor_tensor(y[:], p_bank[:], tz_read[:, :, reads], ALU.add)
+            nc.sync.dma_start(out_rows[:, :, reads], y[:])
+            y_round = sbuf("y_round%d" % h, [P, PACK * HALF], BF16)
+            nc.scalar.copy(woven(y_round[:]), rows_of(y[:]))
+            nc.vector.quantize_mx(out=y_codes[:, reads].bitcast(E4M3), scales=y_exps[:, reads], in_=y_round[:])
+            nc.sync.dma_start(out_codes[:, reads], y_codes[:, reads])
+        for q in range(QUADS):
+            queue = nc.scalar if q % 2 == 0 else nc.sync
+            queue.dma_start(out_2[0, 4 * q : 4 * q + 4, :].bitcast(I32), y_exps[32 * q : 32 * q + 4, :].bitcast(I32))

@@ -42,16 +42,16 @@ def tile_list_crossed_twoboards_one_tabled_pl_kernel(
             nc.sync.dma_start(entries[:], source)
             return entries
 
-        def load_words(name, source, tag=None):
+        def load_words(queue, name, source):
             words = source.bitcast(I32)
-            raw = sbuf(name, [P, words.shape[1]], I32, tag)
-            nc.sync.dma_start(raw[:], words)
+            raw = sbuf(name, [P, words.shape[1]], I32)
+            queue.dma_start(raw[:], words)
             return raw
 
-        def load_scales(plane, source):
-            for q in range(QUADS):
-                queue = nc.scalar if q % 2 == 0 else nc.sync
-                queue.dma_start(plane[32 * q : 32 * q + 4, :].bitcast(I32), source[0, 4 * q : 4 * q + 4, :].bitcast(I32))
+        def load_scales(queue, plane, source, quads=range(QUADS)):
+            for q in quads:
+                rows = source[0, 4 * q : 4 * q + 4, :].bitcast(I32)
+                queue.dma_start(plane[32 * q : 32 * (q + 1), :].bitcast(I32), rows.partition_broadcast(8))
 
         def deal(copy, dealt, raw):
             copy(dealt.rearrange("p (t m) -> p m t", t=PACK), raw.rearrange("p (m t) -> p m t", t=PACK))
@@ -60,32 +60,38 @@ def tile_list_crossed_twoboards_one_tabled_pl_kernel(
         xo_plane = sbuf("xo_plane", [P, Z], U8)
         ww_plane = sbuf("ww_plane", [P, 2 * R], U8)
         wb_plane = sbuf("wb_plane", [P, N], U8)
-        for plane in (xt_plane, ww_plane, xo_plane, wb_plane):
-            nc.vector.memset(plane[:].bitcast(I32), 0)
+        wb_raw = load_words(nc.gpsimd, "wb_raw", wb_words[0])
 
-        xt_raw = load_words("xt_raw", xt_words[0].rearrange("p c b -> p (c b)"), "wide0")
         idx = load_list("idx", offs)
-        w2_raw = load_words("w2_raw", w2_words[0].rearrange("p c b -> p (c b)"), "wide2")
-        w_raw = load_words("w_raw", w_words[0], "wide3")
-        load_scales(xt_plane[:], xt_scales)
-        load_scales(ww_plane[:, 0:R], w_scales)
-        load_scales(ww_plane[:, R : 2 * R], w2_scales)
-        xo_raw = load_words("xo_raw", xo_words[0].rearrange("p c b -> p (c b)"), "wide1")
+        load_scales(nc.sync, xt_plane[:], xt_scales)
+        load_scales(nc.sync, ww_plane[:, 0:R], w_scales, range(0, 2))
+        xt_raw = load_words(nc.sync, "xt_raw", xt_words[0].rearrange("p c b -> p (c b)"))
+        load_scales(nc.sync, ww_plane[:, 0:R], w_scales, range(2, QUADS))
+        load_scales(nc.sync, ww_plane[:, R : 2 * R], w2_scales, range(0, 2))
+        w2_raw = load_words(nc.sync, "w2_raw", w2_words[0].rearrange("p c b -> p (c b)"))
+        w_raw = load_words(nc.sync, "w_raw", w_words[0])
+        xo_raw = load_words(nc.sync, "xo_raw", xo_words[0].rearrange("p c b -> p (c b)"))
+        load_scales(nc.sync, ww_plane[:, R : 2 * R], w2_scales, range(2, QUADS))
         idx2 = load_list("idx2", offs2)
-        load_scales(xo_plane[:], xo_scales)
-        idx3 = load_list("idx3", offs3)
+        load_scales(nc.sync, xo_plane[:], xo_scales)
         idx4 = load_list("idx4", offs4)
+        idx3 = load_list("idx3", offs3)
         idx5 = load_list("idx5", offs5)
         idx6 = load_list("idx6", offs6)
-        wb_raw = load_words("wb_raw", wb_words[0])
-        load_scales(wb_plane[:], wb_scales)
         idx7 = load_list("idx7", offs7)
+        load_scales(nc.sync, wb_plane[:], wb_scales)
+        tz_rows = tz.rearrange("(p t) e -> p t e", t=PACK)
+        tz_raw = []
+        for t in range(PACK):
+            rows = sbuf("tz_raw%d" % t, [P, E], F32)
+            nc.sync.dma_start(rows[:], tz_rows[:, t, :])
+            tz_raw.append(rows)
 
         pw = [sbuf("pw%d" % t, [P, C], F32) for t in range(PACK)]
         pv = [sbuf("pv%d" % t, [P, C], F32) for t in range(PACK)]
         for t in range(PACK):
             nc.vector.memset(pv[t][:], 0.0)
-            nc.vector.memset(pw[t][:], 0.0)
+            nc.gpsimd.memset(pw[t][:], 0.0)
 
         w_codes = sbuf("w_codes", [P, 2 * R], U8)
         w2_codes = sbuf("w2_codes", [P, R], U32)
@@ -99,19 +105,10 @@ def tile_list_crossed_twoboards_one_tabled_pl_kernel(
         xo_exps = sbuf("xo_exps", [P, J], U8)
         nc.vector.tensor_copy(xt_codes[:], xt_raw[:].bitcast(U32).indirect(idx[:]))
         nc.vector.tensor_copy(xt_exps[:], xt_plane[:].indirect(idx[:]))
-        nc.vector.tensor_copy(
-            ww_exps[:].rearrange("p (u t m) -> p u m t", u=2, t=PACK),
-            ww_plane[:].rearrange("p (u m t) -> p u m t", u=2, t=PACK),
-        )
+        deal(nc.vector.tensor_copy, ww_exps[:, 0:R], ww_plane[:, 0:R])
         nc.vector.tensor_copy(xo_codes[:], xo_raw[:].bitcast(U32).indirect(idx2[:]))
+        deal(nc.vector.tensor_copy, ww_exps[:, R : 2 * R], ww_plane[:, R : 2 * R])
         nc.vector.tensor_copy(xo_exps[:], xo_plane[:].indirect(idx2[:]))
-
-        tz_rows = tz.rearrange("(p t) e -> p t e", t=PACK)
-        tz_raw = []
-        for t in range(PACK):
-            rows = sbuf("tz_raw%d" % t, [P, E], F32, "wide%d" % t)
-            nc.sync.dma_start(rows[:], tz_rows[:, t, :])
-            tz_raw.append(rows)
 
         xt_operand = (xt_codes[:].bitcast(E5M2), xt_exps[:])
         xo_operand = (xo_codes[:].bitcast(E4M3), xo_exps[:])
@@ -124,9 +121,7 @@ def tile_list_crossed_twoboards_one_tabled_pl_kernel(
 
         pw_read = sbuf("pw_read", [P, PACK, O], F32)
         diff = sbuf("diff", [P, PACK, O], F32)
-        tz_read = sbuf("tz_read", [P, PACK, O], F32)
         wb_codes = sbuf("wb_codes", [P, 2 * N], U8)
-        wb_exps = sbuf("wb_exps", [P, N], U8)
 
         def read_boards(t, first, count):
             columns = slice(first // PER_COLUMN, (first + count) // PER_COLUMN)
@@ -145,17 +140,27 @@ def tile_list_crossed_twoboards_one_tabled_pl_kernel(
             product(a_bank[:], w2_slice, xo_operand, False, True)
             a_sums = sbuf("a_sums%d" % t, [P, J], F32)
             b_sums = sbuf("b_sums%d" % t, [P, J], F32)
-            nc.scalar.activation(b_sums[:], b_bank[:], ACT.Copy)
+            nc.vector.tensor_copy(b_sums[:], b_bank[:])
             nc.scalar.activation(a_sums[:], a_bank[:], ACT.Copy)
+            if t > 0:
+                read_boards(t - 1, 0, O)
             nc.vector.tensor_copy(pv[t][:].indirect(idx4[:]), b_sums[:])
             nc.scalar.activation(pw[t][:].indirect(idx3[:]), a_sums[:], ACT.Copy)
-            if t < PACK - 1:
-                read_boards(t, 0, O)
 
         deal(nc.scalar.copy, wb_codes[:].bitcast(U16), wb_raw[:].bitcast(U16))
+        wb_exps = sbuf("wb_exps", [P, N], U8, "b_sums1")
         deal(nc.vector.tensor_copy, wb_exps[:], wb_plane[:])
-        for t in range(PACK):
-            nc.vector.tensor_copy(tz_read[:, t, :], tz_raw[t][:].indirect(idx7[:]))
+
+        def read_table(on_vector, entries, t, h):
+            window = tz_raw[t][:].indirect(idx7[:, h * HALF // PER_COLUMN : (h + 1) * HALF // PER_COLUMN])
+            if on_vector:
+                nc.vector.tensor_copy(entries[:, t, :], window)
+            else:
+                nc.scalar.activation(entries[:, t, :], window, ACT.Copy)
+
+        tz_read = [pw_read[:, :, HALF:O], diff[:, :, HALF:O]]
+        for t in range(PACK - 1):
+            read_table(False, tz_read[0], t, 0)
 
         def woven(tile_ap):
             return tile_ap.rearrange("p (c i t) -> p c t i", i=4, t=PACK)
@@ -171,6 +176,8 @@ def tile_list_crossed_twoboards_one_tabled_pl_kernel(
         out_codes = out_1[0].rearrange("p c b -> p (c b)").bitcast(I32)
         for h in range(HALVES):
             read_boards(PACK - 1, h * HALF, HALF)
+        read_table(True, tz_read[0], PACK - 1, 0)
+        p_banks = []
         for h in range(HALVES):
             reads = slice(h * HALF, (h + 1) * HALF)
             hid = sbuf("hid%d" % h, [P, PACK * HALF], BF16)
@@ -181,11 +188,17 @@ def tile_list_crossed_twoboards_one_tabled_pl_kernel(
             for t in range(PACK):
                 wb_slice = (wb_codes[:, 2 * P * t : 2 * P * (t + 1)].bitcast(E2M1), wb_exps[:, P * t : P * (t + 1)])
                 product(p_bank[:, t, :], wb_slice, hid_operand, True, True)
+            p_banks.append(p_bank)
+        for t in range(PACK):
+            read_table(t == PACK - 1, tz_read[1], t, 1)
+        for h in range(HALVES):
+            reads = slice(h * HALF, (h + 1) * HALF)
             y = sbuf("y%d" % h, [P, PACK, HALF], F32)
-            nc.vector.tensor_tensor(y[:], p_bank[:], tz_read[:, :, reads], ALU.add)
+            nc.vector.tensor_tensor(y[:], p_banks[h][:], tz_read[h], ALU.add)
             nc.sync.dma_start(out_rows[:, :, reads], y[:])
             y_round = sbuf("y_round%d" % h, [P, PACK * HALF], BF16)
-            nc.scalar.copy(woven(y_round[:]), rows_of(y[:]))
+            rounding = nc.scalar.copy if h == 0 else nc.vector.tensor_copy
+            rounding(woven(y_round[:]), rows_of(y[:]))
             nc.vector.quantize_mx(out=y_codes[:, reads].bitcast(E4M3), scales=y_exps[:, reads], in_=y_round[:])
             nc.sync.dma_start(out_codes[:, reads], y_codes[:, reads])
         for q in range(QUADS):

from contextlib import ExitStack

import concourse.mybir as mybir

K, T, Z, J, R, C, O, N, E = 512, 1024, 1024, 256, 512, 512, 256, 512, 1024
FLOPS = 2 * K * R * J * 4 + 2 * R * N * O

F32 = mybir.dt.float32
BF16 = mybir.dt.bfloat16
I32 = mybir.dt.int32
U32 = mybir.dt.uint32
U16 = mybir.dt.uint16
U8 = mybir.dt.uint8
E4M3 = mybir.dt.float8_e4m3fn_x4
E5M2 = mybir.dt.float8_e5m2_x4
E2M1 = mybir.dt.float4_e2m1fn_x4
ACT = mybir.ActivationFunctionType
ALU = mybir.AluOpType

P = 128
PACK = 4
QUADS = 4
HALVES = 2
HALF = O // HALVES
PER_COLUMN = 16


def tile_list_crossed_twoboards_one_tabled_pl_kernel(
    tc, xt_words, xt_scales, xo_words, xo_scales, w_words, w_scales, w2_words, w2_scales,
    wb_words, wb_scales, tz, offs, offs2, offs3, offs4, offs5, offs6, offs7, out_0, out_1, out_2,
):
    nc = tc.nc
    with ExitStack() as ctx:
        held = ctx.enter_context(tc.tile_pool(name="held", bufs=1))
        psum = ctx.enter_context(tc.psum_pool(name="psum", bufs=1))

        def sbuf(name, shape, dtype, tag=None):
            return held.tile(shape, dtype, name=name, tag=tag or name, align_bytes=64)

        def load_list(name, source):
            entries = held.tile([P, J // PER_COLUMN], U16, name=name)
            nc.sync.dma_start(entries[:], source)
            return entries

        def load_words(queue, name, source):
            words = source.bitcast(I32)
            raw = sbuf(name, [P, words.shape[1]], I32)
            queue.dma_start(raw[:], words)
            return raw

        def load_scales(queue, plane, source, quads=range(QUADS)):
            for q in quads:
                rows = source[0, 4 * q : 4 * q + 4, :].bitcast(I32)
                queue.dma_start(plane[32 * q : 32 * (q + 1), :].bitcast(I32), rows.partition_broadcast(8))

        def deal(copy, dealt, raw):
            copy(dealt.rearrange("p (t m) -> p m t", t=PACK), raw.rearrange("p (m t) -> p m t", t=PACK))

        xt_plane = sbuf("xt_plane", [P, T], U8)
        xo_plane = sbuf("xo_plane", [P, Z], U8)
        ww_plane = sbuf("ww_plane", [P, 2 * R], U8)
        wb_plane = sbuf("wb_plane", [P, N], U8)
        wb_raw = load_words(nc.gpsimd, "wb_raw", wb_words[0])

        idx = load_list("idx", offs)
        load_scales(nc.sync, xt_plane[:], xt_scales)
        load_scales(nc.sync, ww_plane[:, 0:R], w_scales, range(0, 2))
        xt_raw = load_words(nc.sync, "xt_raw", xt_words[0].rearrange("p c b -> p (c b)"))
        load_scales(nc.sync, ww_plane[:, 0:R], w_scales, range(2, QUADS))
        load_scales(nc.sync, ww_plane[:, R : 2 * R], w2_scales, range(0, 2))
        w2_raw = load_words(nc.sync, "w2_raw", w2_words[0].rearrange("p c b -> p (c b)"))
        w_raw = load_words(nc.sync, "w_raw", w_words[0])
        xo_raw = load_words(nc.sync, "xo_raw", xo_words[0].rearrange("p c b -> p (c b)"))
        load_scales(nc.sync, ww_plane[:, R : 2 * R], w2_scales, range(2, QUADS))
        idx2 = load_list("idx2", offs2)
        load_scales(nc.sync, xo_plane[:], xo_scales)
        idx4 = load_list("idx4", offs4)
        idx3 = load_list("idx3", offs3)
        idx5 = load_list("idx5", offs5)
        idx6 = load_list("idx6", offs6)
        idx7 = load_list("idx7", offs7)
        load_scales(nc.sync, wb_plane[:], wb_scales)
        tz_rows = tz.rearrange("(p t) e -> p t e", t=PACK)
        tz_raw = []
        for t in range(PACK):
            rows = sbuf("tz_raw%d" % t, [P, E], F32)
            nc.sync.dma_start(rows[:], tz_rows[:, t, :])
            tz_raw.append(rows)

        pw = [sbuf("pw%d" % t, [P, C], F32) for t in range(PACK)]
        pv = [sbuf("pv%d" % t, [P, C], F32) for t in range(PACK)]
        for t in range(PACK):
            nc.vector.memset(pv[t][:], 0.0)
            nc.gpsimd.memset(pw[t][:], 0.0)

        w_codes = sbuf("w_codes", [P, 2 * R], U8)
        w2_codes = sbuf("w2_codes", [P, R], U32)
        ww_exps = sbuf("ww_exps", [P, 2 * R], U8)
        deal(nc.scalar.copy, w2_codes[:], w2_raw[:].bitcast(U32))
        deal(nc.scalar.copy, w_codes[:].bitcast(U16), w_raw[:].bitcast(U16))

        xt_codes = sbuf("xt_codes", [P, J], U32)
        xt_exps = sbuf("xt_exps", [P, J], U8)
        xo_codes = sbuf("xo_codes", [P, J], U32)
        xo_exps = sbuf("xo_exps", [P, J], U8)
        nc.vector.tensor_copy(xt_codes[:], xt_raw[:].bitcast(U32).indirect(idx[:]))
        nc.vector.tensor_copy(xt_exps[:], xt_plane[:].indirect(idx[:]))
        deal(nc.vector.tensor_copy, ww_exps[:, 0:R], ww_plane[:, 0:R])
        nc.vector.tensor_copy(xo_codes[:], xo_raw[:].bitcast(U32).indirect(idx2[:]))
        deal(nc.vector.tensor_copy, ww_exps[:, R : 2 * R], ww_plane[:, R : 2 * R])
        nc.vector.tensor_copy(xo_exps[:], xo_plane[:].indirect(idx2[:]))

        xt_operand = (xt_codes[:].bitcast(E5M2), xt_exps[:])
        xo_operand = (xo_codes[:].bitcast(E4M3), xo_exps[:])

        def product(bank, stationary, moving, start, stop):
            nc.tensor.matmul_mx(
                out=bank, lhsT=stationary[0], lhsT_scale=stationary[1],
                rhs=moving[0], rhs_scale=moving[1], start=start, stop=stop,
            )

        pw_read = sbuf("pw_read", [P, PACK, O], F32)
        diff = sbuf("diff", [P, PACK, O], F32)
        wb_codes = sbuf("wb_codes", [P, 2 * N], U8)

        def read_boards(t, first, count):
            columns = slice(first // PER_COLUMN, (first + count) // PER_COLUMN)
            reads = slice(first, first + count)
            nc.scalar.activation(pw_read[:, t, reads], pw[t][:].indirect(idx5[:, columns]), ACT.Copy)
            nc.vector.tensor_tensor(diff[:, t, reads], pv[t][:].indirect(idx6[:, columns]), pw_read[:, t, reads], ALU.subtract)

        for t in range(PACK):
            w_slice = (w_codes[:, 2 * P * t : 2 * P * (t + 1)].bitcast(E2M1), ww_exps[:, P * t : P * (t + 1)])
            w2_slice = (w2_codes[:, P * t : P * (t + 1)].bitcast(E5M2), ww_exps[:, R + P * t : R + P * (t + 1)])
            a_bank = psum.tile([P, J], F32, name="a_bank%d" % t, tag="bank%d" % (2 * t))
            b_bank = psum.tile([P, J], F32, name="b_bank%d" % t, tag="bank%d" % (2 * t + 1))
            product(b_bank[:], w2_slice, xt_operand, True, False)
            product(a_bank[:], w_slice, xt_operand, True, False)
            product(b_bank[:], w_slice, xo_operand, False, True)
            product(a_bank[:], w2_slice, xo_operand, False, True)
            a_sums = sbuf("a_sums%d" % t, [P, J], F32)
            b_sums = sbuf("b_sums%d" % t, [P, J], F32)
            nc.vector.tensor_copy(b_sums[:], b_bank[:])
            nc.scalar.activation(a_sums[:], a_bank[:], ACT.Copy)
            if t > 0:
                read_boards(t - 1, 0, O)
            nc.vector.tensor_copy(pv[t][:].indirect(idx4[:]), b_sums[:])
            nc.scalar.activation(pw[t][:].indirect(idx3[:]), a_sums[:], ACT.Copy)

        deal(nc.scalar.copy, wb_codes[:].bitcast(U16), wb_raw[:].bitcast(U16))
        wb_exps = sbuf("wb_exps", [P, N], U8, "b_sums1")
        deal(nc.vector.tensor_copy, wb_exps[:], wb_plane[:])

        def read_table(on_vector, entries, t, h):
            window = tz_raw[t][:].indirect(idx7[:, h * HALF // PER_COLUMN : (h + 1) * HALF // PER_COLUMN])
            if on_vector:
                nc.vector.tensor_copy(entries[:, t, :], window)
            else:
                nc.scalar.activation(entries[:, t, :], window, ACT.Copy)

        tz_read = [pw_read[:, :, HALF:O], diff[:, :, HALF:O]]
        for t in range(PACK - 1):
            read_table(False, tz_read[0], t, 0)

        def woven(tile_ap):
            return tile_ap.rearrange("p (c i t) -> p c t i", i=4, t=PACK)

        def rows_of(slices_ap):
            return slices_ap.rearrange("p t (c i) -> p c t i", i=4)

        hid_codes = sbuf("hid_codes", [P, O], U32)
        hid_exps = sbuf("hid_exps", [P, O], U8)
        y_codes = sbuf("y_codes", [P, O], I32)
        y_exps = sbuf("y_exps", [P, O], U8)
        out_rows = out_0.rearrange("(p t) o -> p t o", t=PACK)
        out_codes = out_1[0].rearrange("p c b -> p (c b)").bitcast(I32)
        for h in range(HALVES):
            read_boards(PACK - 1, h * HALF, HALF)
        read_table(True, tz_read[0], PACK - 1, 0)
        p_banks = []
        for h in range(HALVES):
            reads = slice(h * HALF, (h + 1) * HALF)
            hid = sbuf("hid%d" % h, [P, PACK * HALF], BF16)
            nc.scalar.activation(woven(hid[:]), rows_of(diff[:, :, reads]), ACT.Abs)
            nc.vector.quantize_mx(out=hid_codes[:, reads].bitcast(E4M3), scales=hid_exps[:, reads], in_=hid[:])
            p_bank = psum.tile([P, PACK, HALF], F32, name="p_bank%d" % h, tag="bank%d" % h)
            hid_operand = (hid_codes[:, reads].bitcast(E4M3), hid_exps[:, reads])
            for t in range(PACK):
                wb_slice = (wb_codes[:, 2 * P * t : 2 * P * (t + 1)].bitcast(E2M1), wb_exps[:, P * t : P * (t + 1)])
                product(p_bank[:, t, :], wb_slice, hid_operand, True, True)
            p_banks.append(p_bank)
        for t in range(PACK):
            read_table(t == PACK - 1, tz_read[1], t, 1)
        for h in range(HALVES):
            reads = slice(h * HALF, (h + 1) * HALF)
            y = sbuf("y%d" % h, [P, PACK, HALF], F32)
            nc.vector.tensor_tensor(y[:], p_banks[h][:], tz_read[h], ALU.add)
            nc.sync.dma_start(out_rows[:, :, reads], y[:])
            y_round = sbuf("y_round%d" % h, [P, PACK * HALF], BF16)
            rounding = nc.scalar.copy if h == 0 else nc.vector.tensor_copy
            rounding(woven(y_round[:]), rows_of(y[:]))
            nc.vector.quantize_mx(out=y_codes[:, reads].bitcast(E4M3), scales=y_exps[:, reads], in_=y_round[:])
            nc.sync.dma_start(out_codes[:, reads], y_codes[:, reads])
        for q in range(QUADS):
            queue = nc.scalar if q % 2 == 0 else nc.sync
            queue.dma_start(out_2[0, 4 * q : 4 * q + 4, :].bitcast(I32), y_exps[32 * q : 32 * q + 4, :].bitcast(I32))
